import numpy as np
import ml_dtypes


def mxq(x, axis, fmt="e4m3"):
    dtype, down = {"e4m3": (ml_dtypes.float8_e4m3fn, 7), "e5m2": (ml_dtypes.float8_e5m2, 14)}[fmt]
    v = np.moveaxis(np.asarray(x, np.float32).astype(ml_dtypes.bfloat16).astype(np.float64), axis, -1)
    blocks = v.reshape(v.shape[:-1] + (-1, 32))
    amax = np.abs(blocks).max(-1, keepdims=True)
    byte = np.maximum(np.where(amax > 0, np.frexp(amax)[1] - 1 + 127, 0) - down, 1)
    scale = np.exp2(byte - 127.0)
    codes = (blocks / scale).astype(np.float32).astype(dtype).astype(np.float64)
    return np.moveaxis((codes * scale).reshape(v.shape), -1, axis)


WIDE = False


def mx_kscale(k):
    if not WIDE:
        return np.ones(k)
    levels = np.array([10, -10, 5, -5, 0])
    if k % 512:
        return np.exp2(np.random.permutation(np.resize(levels, k // 32))).repeat(32)
    a = np.empty((k // 512, 16))
    for p in range(k // 512):
        a[p, :8] = np.random.permutation(np.resize(levels, 8))
        for g in range(8):
            far = levels[np.abs(levels - a[p, g]) >= 10]
            a[p, g + 8] = far[np.random.randint(len(far))]
    return np.exp2(a.ravel()).repeat(32)


def f64(x):
    return np.asarray(x).astype(np.float64)


def striped8(idx):
    return np.asarray(idx).reshape(8, -1, 16).transpose(0, 2, 1).reshape(128, -1).astype(np.uint16)


def unstriped8(offs):
    return offs.reshape(8, 16, -1).transpose(0, 2, 1).reshape(8, -1).astype(np.int64)


def pick8(x, idx, run):
    r = np.arange(len(x))
    return x[r[:, None], idx[r % (8 * run) // run]]


E2M1 = np.array([0.0, 0.5, 1.0, 1.5, 2.0, 3.0, 4.0, 6.0, -0.0, -0.5, -1.0, -1.5, -2.0, -3.0, -4.0, -6.0])


def pack_weight(w, fmt):
    k, n = w.shape
    w = f64(np.asarray(w, np.float32).astype(ml_dtypes.bfloat16)).reshape(k // 32, 32, n)
    amax = np.abs(w).max(1)
    if fmt == "e4m3":
        byte = np.frexp(amax)[1] - 1 + 127 - 7
    else:
        mant, ex = np.frexp(amax / 6.0)
        byte = np.where(mant > 0.5, ex, ex - 1) + 127
    byte = np.clip(np.where(amax > 0, byte, 1), 1, 254)
    scaled = (w * np.exp2(127.0 - byte)[:, None, :]).reshape(k, n).astype(np.float32)
    by_word = np.ascontiguousarray(scaled.reshape(k // 512, 128, 4, n).transpose(0, 1, 3, 2))
    if fmt == "e4m3":
        words = by_word.astype(ml_dtypes.float8_e4m3fn).view(np.uint8)
    else:
        c = by_word.astype(ml_dtypes.float4_e2m1fn).view(np.uint8) & 0xF
        words = (c[..., 0::2] | (c[..., 1::2] << 4)).reshape(k // 512, 128, 2 * n)
    return np.ascontiguousarray(words), np.ascontiguousarray(byte.astype(np.uint8).reshape(k // 512, 16, n))


def unpack_weight(words, scales, fmt):
    g, _, n = scales.shape
    words = np.ascontiguousarray(words).reshape(g, 128, n, -1)
    if fmt == "e4m3":
        vals = words.view(ml_dtypes.float8_e4m3fn).astype(np.float64)
    else:
        nib = np.empty((g, 128, n, 4), np.uint8)
        nib[..., 0::2] = words & 0xF
        nib[..., 1::2] = words >> 4
        vals = E2M1[nib]
    vals = vals * np.repeat(np.exp2(scales.astype(np.float64) - 127.0), 8, axis=1)[..., None]
    return vals.transpose(0, 1, 3, 2).reshape(g * 512, n)


def sigmoid(v):
    return 1.0 / (1.0 + np.exp(-v))


D, K, T, U, X, I, Q = 512, 512, 1024, 1024, 1024, 512, 128


def setup_inputs():
    n = np.random.standard_normal
    idx = np.stack([np.random.permutation(T)[:I] for _ in range(8)])
    idx2 = np.stack([np.random.permutation(U)[:I] for _ in range(8)])
    idx3 = np.stack([np.random.permutation(X)[:I] for _ in range(8)])
    idx4 = np.stack([np.random.permutation(X)[:I] for _ in range(8)])
    fd = mx_kscale(D)
    fk = mx_kscale(K)
    wqp = pack_weight(n((D, K)) * 1.0 / np.sqrt(D) * fd[:, None] * fk, "e4m3")
    keysp = pack_weight(n((K, T)) * 1.0 / np.sqrt(K) / fk[:, None], "e4m3")
    notesp = pack_weight(n((K, U)) * 1.0 / np.sqrt(K) / fk[:, None], "e2m1")
    usersp = pack_weight(n((D, X)) * 1.0 / np.sqrt(D) * fd[:, None], "e4m3")
    return {
        "states": (n((D, Q)) * 0.95 / fd[:, None]).astype(np.float32),
        "wq_words": wqp[0],
        "wq_scales": wqp[1],
        "keys_words": keysp[0],
        "keys_scales": keysp[1],
        "notes_words": notesp[0],
        "notes_scales": notesp[1],
        "users_words": usersp[0],
        "users_scales": usersp[1],
        "thr": (np.random.uniform(-0.6, 0.6, (Q, 1))).astype(np.float32),
        "slope": (np.random.uniform(1.0, 3.0, (Q, 1))).astype(np.float32),
        "offs": striped8(idx),
        "offs2": striped8(idx2),
        "offs3": striped8(idx3),
        "offs4": striped8(idx4),
    }


def reference(states, wq_words, wq_scales, keys_words, keys_scales, notes_words, notes_scales, users_words, users_scales, thr, slope, offs, offs2, offs3, offs4):
    idx = unstriped8(offs)
    idx2 = unstriped8(offs2)
    idx3 = unstriped8(offs3)
    idx4 = unstriped8(offs4)
    wqu = unpack_weight(wq_words, wq_scales, "e4m3")
    keysu = unpack_weight(keys_words, keys_scales, "e4m3")
    notesu = unpack_weight(notes_words, notes_scales, "e2m1")
    usersu = unpack_weight(users_words, users_scales, "e4m3")
    statesq = mxq(f64(states), 0, "e4m3")
    qv = wqu.T @ statesq
    qvq = mxq(qv, 0, "e4m3")
    a = qvq.T @ keysu
    b = qvq.T @ notesu
    c0 = statesq.T @ usersu
    s1 = sigmoid(pick8(a, idx, 16) * f64(slope) + f64(thr))
    s2 = sigmoid(pick8(b, idx2, 16) * f64(slope) + f64(thr))
    r = s1 - s2
    f1 = np.zeros((Q, X))
    f1[np.arange(Q)[:, None], idx3[np.arange(Q) % 128 // 16]] = r
    cc = c0 + f1 * 3.0
    y = pick8(cc, idx4, 16)
    return y

@@ -1,0 +1,208 @@
+from contextlib import ExitStack
+
+import concourse.mybir as mybir
+
+FLOPS = 469762048
+
+F32 = mybir.dt.float32
+BF16 = mybir.dt.bfloat16
+I32 = mybir.dt.int32
+U32 = mybir.dt.uint32
+U16 = mybir.dt.uint16
+U8 = mybir.dt.uint8
+FP8X4 = mybir.dt.float8_e4m3fn_x4
+FP4X4 = mybir.dt.float4_e2m1fn_x4
+ALU = mybir.AluOpType
+ACT = mybir.ActivationFunctionType
+
+P = 128
+PACK = 4
+QUADRANT = 32
+K = 512
+Q = 128
+COLS = 1024
+SLOTS = 512
+HALF = SLOTS // 2
+LIST_COLS = SLOTS // 16
+BANK = 512
+NOTE_CHUNK = 256
+KEYS_ROW = 4
+USERS_ROW = 8
+
+
+def load_words(nc, tile, words):
+    nc.sync.dma_start(out=tile[:].bitcast(I32), in_=words.bitcast(I32))
+
+
+def load_scales(queue, plane, scales, first_row):
+    rows = scales[0].rearrange("(g r) n -> r g n", r=PACK)
+    for r in range(PACK):
+        queue.dma_start(
+            out=plane[first_row + r : P : QUADRANT, :].bitcast(I32), in_=rows[r].bitcast(I32)
+        )
+
+
+def tile_attend_gatedgap_madethree_kernel(
+    tc, states, wq_words, wq_scales, keys_words, keys_scales, notes_words, notes_scales,
+    users_words, users_scales, thr, slope, offs, offs2, offs3, offs4, out,
+):
+    nc = tc.nc
+    with ExitStack() as ctx:
+        sb = ctx.enter_context(tc.tile_pool(name="sb", bufs=1))
+        ps = ctx.enter_context(tc.psum_pool(name="ps", bufs=1))
+
+        wq_w = [sb.tile([P, K // 2], U32, name="wq_w%d" % h, align_bytes=64) for h in range(2)]
+        wq_s = sb.tile([P, K], U8, name="wq_s", align_bytes=64)
+        wq_wd = sb.tile([P, K], U32, name="wq_wd", align_bytes=64)
+        wq_sd = sb.tile([P, K], U8, name="wq_sd", align_bytes=64)
+        keys_w = sb.tile([P, COLS], U32, name="keys_w", align_bytes=64)
+        keys_s = sb.tile([P, COLS], U8, name="keys_s", align_bytes=64)
+        notes_w = sb.tile([P, 2 * COLS], U8, name="notes_w", align_bytes=64)
+        notes_s = sb.tile([P, COLS], U8, name="notes_s", align_bytes=64)
+        users_w = sb.tile([P, COLS], U32, name="users_w", align_bytes=64)
+        users_s = sb.tile([P, COLS], U8, name="users_s", align_bytes=64)
+        st_raw = sb.tile([P, PACK, Q], F32, name="st_raw", align_bytes=64)
+        st_bf = sb.tile([P, Q, PACK], BF16, name="st_bf", align_bytes=64)
+        st_w = sb.tile([P, Q], U32, name="st_w", align_bytes=64)
+        st_s = sb.tile([P, Q], U8, name="st_s", align_bytes=64)
+        qv_bf = sb.tile([P, Q, PACK], BF16, name="qv_bf", align_bytes=64)
+        qv_w = sb.tile([P, Q], U32, name="qv_w", align_bytes=64)
+        qv_s = sb.tile([P, Q], U8, name="qv_s", align_bytes=64)
+        thr_t = sb.tile([P, 1], F32, name="thr_t")
+        slope_t = sb.tile([P, 1], F32, name="slope_t")
+        list1 = sb.tile([P, LIST_COLS], U16, name="list1")
+        list2 = sb.tile([P, LIST_COLS], U16, name="list2")
+        list3 = sb.tile([P, LIST_COLS], U16, name="list3")
+        list4 = sb.tile([P, LIST_COLS], U16, name="list4")
+        a_sb = sb.tile([P, COLS], F32, name="a_sb")
+        b_sb = sb.tile([P, COLS], F32, name="b_sb")
+        s1 = [sb.tile([P, HALF], F32, name="s1_%d" % h) for h in range(2)]
+        s2 = sb.tile([P, SLOTS], F32, name="s2")
+        s2_neg = sb.tile([P, SLOTS], F32, name="s2_neg")
+        f1 = sb.tile([P, COLS], F32, name="f1")
+        cc = sb.tile([P, COLS], F32, name="cc")
+        y = [sb.tile([P, HALF], F32, name="y_%d" % h) for h in range(2)]
+
+        for plane in (notes_s, keys_s, users_s):
+            nc.vector.memset(plane[:].bitcast(I32), 0)
+        nc.vector.memset(f1[:], 0.0)
+
+        wq_rows = wq_words[0].rearrange("p n t -> p (n t)")
+        nc.sync.dma_start(out=st_raw[:], in_=states.rearrange("(p j) q -> p j q", j=PACK))
+        for g in range(P // QUADRANT):
+            rows = wq_scales[0][PACK * g : PACK * (g + 1), :].bitcast(I32)
+            nc.sync.dma_start(
+                out=wq_s[QUADRANT * g : QUADRANT * (g + 1), :].bitcast(I32),
+                in_=rows.unsqueeze(0).to_broadcast([QUADRANT // PACK, PACK, K // 4]),
+            )
+        load_words(nc, wq_w[0], wq_rows[:, 0 : 2 * K])
+        load_words(nc, wq_w[1], wq_rows[:, 2 * K : 4 * K])
+        load_words(nc, notes_w, notes_words[0])
+        load_words(nc, keys_w, keys_words[0].rearrange("p n t -> p (n t)"))
+        load_scales(nc.sync, notes_s, notes_scales, 0)
+        load_scales(nc.sync, keys_s, keys_scales, KEYS_ROW)
+        nc.gpsimd.dma_start(out=slope_t[:], in_=slope)
+        nc.gpsimd.dma_start(out=thr_t[:], in_=thr)
+        nc.sync.dma_start(list2[:], offs2)
+        nc.sync.dma_start(list1[:], offs)
+        nc.sync.dma_start(list3[:], offs3)
+        load_words(nc, users_w, users_words[0].rearrange("p n t -> p (n t)"))
+        load_scales(nc.sync, users_s, users_scales, USERS_ROW)
+        nc.sync.dma_start(list4[:], offs4)
+
+        dealt = wq_wd[:].rearrange("p (t m) -> p m t", t=PACK)
+        nc.scalar.copy(
+            out=dealt[:, 0 : P // 2, :], in_=wq_w[0][:].rearrange("p (m t) -> p m t", t=PACK)
+        )
+        nc.vector.tensor_copy(
+            out=st_bf[:].rearrange("p (c i) t -> p c t i", i=4),
+            in_=st_raw[:].rearrange("p t (c i) -> p c t i", i=4),
+        )
+        nc.vector.tensor_copy(
+            out=wq_sd[:].rearrange("p (t m) -> p m t", t=PACK),
+            in_=wq_s[:].rearrange("p (m t) -> p m t", t=PACK),
+        )
+        nc.vector.quantize_mx(
+            out=st_w[:].bitcast(FP8X4), scales=st_s[:], in_=st_bf[:].rearrange("p q t -> p (q t)")
+        )
+        nc.vector.tensor_copy(
+            out=dealt[:, P // 2 : P, :].bitcast(I32),
+            in_=wq_w[1][:].bitcast(I32).rearrange("p (m t) -> p m t", t=PACK),
+        )
+
+        qv_ps = ps.tile([P, BANK], F32, name="qv_ps", tag="shared")
+        for t in range(PACK):
+            cols = slice(t * P, (t + 1) * P)
+            nc.tensor.matmul_mx(
+                out=qv_ps[:, cols], lhsT=wq_wd[:, cols].bitcast(FP8X4), lhsT_scale=wq_sd[:, cols],
+                rhs=st_w[:].bitcast(FP8X4), rhs_scale=st_s[:], start=True, stop=True,
+            )
+        nc.scalar.copy(out=qv_bf[:], in_=qv_ps[:].rearrange("p (t q) -> p q t", t=PACK))
+        nc.vector.quantize_mx(
+            out=qv_w[:].bitcast(FP8X4), scales=qv_s[:], in_=qv_bf[:].rearrange("p q t -> p (q t)")
+        )
+
+        for c in range(COLS // NOTE_CHUNK):
+            cols = slice(c * NOTE_CHUNK, (c + 1) * NOTE_CHUNK)
+            b_ps = ps.tile([P, BANK], F32, name="b_ps%d" % c)
+            nc.tensor.matmul_mx(
+                out=b_ps[:, 0:NOTE_CHUNK], lhsT=qv_w[:].bitcast(FP8X4), lhsT_scale=qv_s[:],
+                rhs=notes_w[:, 2 * cols.start : 2 * cols.stop].bitcast(FP4X4),
+                rhs_scale=notes_s[:, cols], start=True, stop=True,
+            )
+            if c % 2 == 0:
+                nc.scalar.copy(out=b_sb[:, cols], in_=b_ps[:, 0:NOTE_CHUNK])
+            else:
+                nc.vector.tensor_copy(out=b_sb[:, cols], in_=b_ps[:, 0:NOTE_CHUNK])
+
+        nc.scalar.activation(
+            out=s2[:], in_=b_sb[:].indirect(list2[:]), func=ACT.Sigmoid,
+            bias=thr_t[:], scale=slope_t[:],
+        )
+
+        for c in range(COLS // NOTE_CHUNK):
+            cols = slice(c * NOTE_CHUNK, (c + 1) * NOTE_CHUNK)
+            a_ps = ps.tile([P, BANK], F32, name="a_ps%d" % c, tag=("a0", "a1", "a2", "shared")[c])
+            nc.tensor.matmul_mx(
+                out=a_ps[:, 0:NOTE_CHUNK], lhsT=qv_w[:].bitcast(FP8X4), lhsT_scale=qv_s[:],
+                rhs=keys_w[:, cols].bitcast(FP8X4), rhs_scale=keys_s[KEYS_ROW:P, cols],
+                start=True, stop=True,
+            )
+            nc.vector.tensor_copy(out=a_sb[:, cols], in_=a_ps[:, 0:NOTE_CHUNK])
+
+        c0_ps = [
+            ps.tile([P, BANK], F32, name="c0_ps0", tag="b_ps0"),
+            ps.tile([P, BANK], F32, name="c0_ps1", tag="b_ps1"),
+        ]
+        for c in range(COLS // BANK):
+            cols = slice(c * BANK, (c + 1) * BANK)
+            nc.tensor.matmul_mx(
+                out=c0_ps[c][:], lhsT=st_w[:].bitcast(FP8X4), lhsT_scale=st_s[:],
+                rhs=users_w[:, cols].bitcast(FP8X4), rhs_scale=users_s[USERS_ROW:P, cols],
+                start=True, stop=True,
+            )
+
+        nc.vector.tensor_scalar_mul(s2_neg[:], s2[:], -1.0)
+
+        for h in range(2):
+            part = slice(h * LIST_COLS // 2, (h + 1) * LIST_COLS // 2)
+            nc.scalar.activation(
+                out=s1[h][:], in_=a_sb[:].indirect(list1[:, part]), func=ACT.Sigmoid,
+                bias=thr_t[:], scale=slope_t[:],
+            )
+            nc.vector.tensor_tensor(
+                f1[:].indirect(list3[:, part]), s1[h][:], s2_neg[:, h * HALF : (h + 1) * HALF], ALU.add
+            )
+
+        for c in range(COLS // BANK):
+            cols = slice(c * BANK, (c + 1) * BANK)
+            nc.vector.scalar_tensor_tensor(
+                out=cc[:, cols], in0=f1[:, cols], scalar=3.0, in1=c0_ps[c][:], op0=ALU.mult, op1=ALU.add
+            )
+
+        nc.vector.tensor_copy(y[0][:], cc[:].indirect(list4[:, 0 : LIST_COLS // 2]))
+        nc.sync.dma_start(out=out[:, 0:HALF], in_=y[0][:])
+        nc.scalar.activation(
+            out=y[1][:], in_=cc[:].indirect(list4[:, LIST_COLS // 2 : LIST_COLS]), func=ACT.Copy
+        )
+        nc.scalar.dma_start(out=out[:, HALF:SLOTS], in_=y[1][:])

@@ -83,6 +83,11 @@ def tile_attend_gatedgap_madethree_kernel(
         cc = sb.tile([P, COLS], F32, name="cc")
         y = [sb.tile([P, HALF], F32, name="y_%d" % h) for h in range(2)]
 
+        warm_in = sb.tile([P, 1], F32, name="warm_in")
+        warm_out = sb.tile([P, 1], F32, name="warm_out")
+        nc.vector.memset(warm_in[:], 0.0)
+        nc.scalar.activation(out=warm_out[:], in_=warm_in[:], func=ACT.Sigmoid)
+
         for plane in (notes_s, keys_s, users_s):
             nc.vector.memset(plane[:].bitcast(I32), 0)
         nc.vector.memset(f1[:], 0.0)

@@ -51,7 +51,7 @@ def tile_attend_gatedgap_madethree_kernel(
         sb = ctx.enter_context(tc.tile_pool(name="sb", bufs=1))
         ps = ctx.enter_context(tc.psum_pool(name="ps", bufs=1))
 
-        wq_w = [sb.tile([P, K // 2], U32, name="wq_w%d" % h, align_bytes=64) for h in range(2)]
+        wq_w = sb.tile([P, K], U32, name="wq_w", align_bytes=64)
         wq_s = sb.tile([P, K], U8, name="wq_s", align_bytes=64)
         wq_wd = sb.tile([P, K], U32, name="wq_wd", align_bytes=64)
         wq_sd = sb.tile([P, K], U8, name="wq_sd", align_bytes=64)
@@ -77,18 +77,18 @@ def tile_attend_gatedgap_madethree_kernel(
         a_sb = sb.tile([P, COLS], F32, name="a_sb")
         b_sb = sb.tile([P, COLS], F32, name="b_sb")
         s1 = [sb.tile([P, HALF], F32, name="s1_%d" % h) for h in range(2)]
-        s2 = sb.tile([P, SLOTS], F32, name="s2")
-        s2_neg = sb.tile([P, SLOTS], F32, name="s2_neg")
+        s2_neg = [sb.tile([P, HALF], F32, name="s2_neg_%d" % h) for h in range(2)]
         f1 = sb.tile([P, COLS], F32, name="f1")
         cc = sb.tile([P, COLS], F32, name="cc")
         y = [sb.tile([P, HALF], F32, name="y_%d" % h) for h in range(2)]
 
         warm_in = sb.tile([P, 1], F32, name="warm_in")
         warm_out = sb.tile([P, 1], F32, name="warm_out")
+        nc.vector.memset(notes_s[:].bitcast(I32), 0)
         nc.vector.memset(warm_in[:], 0.0)
         nc.scalar.activation(out=warm_out[:], in_=warm_in[:], func=ACT.Sigmoid)
 
-        for plane in (notes_s, keys_s, users_s):
+        for plane in (keys_s, users_s):
             nc.vector.memset(plane[:].bitcast(I32), 0)
         nc.vector.memset(f1[:], 0.0)
 
@@ -100,11 +100,10 @@ def tile_attend_gatedgap_madethree_kernel(
                 out=wq_s[QUADRANT * g : QUADRANT * (g + 1), :].bitcast(I32),
                 in_=rows.unsqueeze(0).to_broadcast([QUADRANT // PACK, PACK, K // 4]),
             )
-        load_words(nc, wq_w[0], wq_rows[:, 0 : 2 * K])
-        load_words(nc, wq_w[1], wq_rows[:, 2 * K : 4 * K])
+        load_words(nc, wq_w, wq_rows)
         load_words(nc, notes_w, notes_words[0])
-        load_words(nc, keys_w, keys_words[0].rearrange("p n t -> p (n t)"))
         load_scales(nc.sync, notes_s, notes_scales, 0)
+        load_words(nc, keys_w, keys_words[0].rearrange("p n t -> p (n t)"))
         load_scales(nc.sync, keys_s, keys_scales, KEYS_ROW)
         nc.gpsimd.dma_start(out=slope_t[:], in_=slope)
         nc.gpsimd.dma_start(out=thr_t[:], in_=thr)
@@ -116,12 +115,13 @@ def tile_attend_gatedgap_madethree_kernel(
         nc.sync.dma_start(list4[:], offs4)
 
         dealt = wq_wd[:].rearrange("p (t m) -> p m t", t=PACK)
+        for engine_copy, rows in ((nc.vector.tensor_copy, slice(0, Q // 2)), (nc.scalar.copy, slice(Q // 2, Q))):
+            engine_copy(
+                out=st_bf[:, rows, :].rearrange("p (c i) t -> p c t i", i=4),
+                in_=st_raw[:, :, rows].rearrange("p t (c i) -> p c t i", i=4),
+            )
         nc.scalar.copy(
-            out=dealt[:, 0 : P // 2, :], in_=wq_w[0][:].rearrange("p (m t) -> p m t", t=PACK)
-        )
-        nc.vector.tensor_copy(
-            out=st_bf[:].rearrange("p (c i) t -> p c t i", i=4),
-            in_=st_raw[:].rearrange("p t (c i) -> p c t i", i=4),
+            out=dealt[:, 0 : P // 2, :], in_=wq_w[:, 0 : K // 2].rearrange("p (m t) -> p m t", t=PACK)
         )
         nc.vector.tensor_copy(
             out=wq_sd[:].rearrange("p (t m) -> p m t", t=PACK),
@@ -132,7 +132,7 @@ def tile_attend_gatedgap_madethree_kernel(
         )
         nc.vector.tensor_copy(
             out=dealt[:, P // 2 : P, :].bitcast(I32),
-            in_=wq_w[1][:].bitcast(I32).rearrange("p (m t) -> p m t", t=PACK),
+            in_=wq_w[:, K // 2 : K].bitcast(I32).rearrange("p (m t) -> p m t", t=PACK),
         )
 
         qv_ps = ps.tile([P, BANK], F32, name="qv_ps", tag="shared")
@@ -160,10 +160,16 @@ def tile_attend_gatedgap_madethree_kernel(
             else:
                 nc.vector.tensor_copy(out=b_sb[:, cols], in_=b_ps[:, 0:NOTE_CHUNK])
 
-        nc.scalar.activation(
-            out=s2[:], in_=b_sb[:].indirect(list2[:]), func=ACT.Sigmoid,
-            bias=thr_t[:], scale=slope_t[:],
-        )
+        parts = [slice(h * LIST_COLS // 2, (h + 1) * LIST_COLS // 2) for h in range(2)]
+
+        def gate(dst, window, offsets):
+            nc.scalar.activation(
+                out=dst[:], in_=window[:].indirect(offsets), func=ACT.Sigmoid,
+                bias=thr_t[:], scale=slope_t[:],
+            )
+
+        s2 = sb.tile([P, HALF], F32, name="s2", tag="s2")
+        gate(s2, b_sb, list2[:, parts[0]])
 
         for c in range(COLS // NOTE_CHUNK):
             cols = slice(c * NOTE_CHUNK, (c + 1) * NOTE_CHUNK)
@@ -173,7 +179,10 @@ def tile_attend_gatedgap_madethree_kernel(
                 rhs=keys_w[:, cols].bitcast(FP8X4), rhs_scale=keys_s[KEYS_ROW:P, cols],
                 start=True, stop=True,
             )
-            nc.vector.tensor_copy(out=a_sb[:, cols], in_=a_ps[:, 0:NOTE_CHUNK])
+            if c == COLS // NOTE_CHUNK - 1:
+                nc.scalar.copy(out=a_sb[:, cols], in_=a_ps[:, 0:NOTE_CHUNK])
+            else:
+                nc.vector.tensor_copy(out=a_sb[:, cols], in_=a_ps[:, 0:NOTE_CHUNK])
 
         c0_ps = [
             ps.tile([P, BANK], F32, name="c0_ps0", tag="b_ps0"),
@@ -187,17 +196,15 @@ def tile_attend_gatedgap_madethree_kernel(
                 start=True, stop=True,
             )
 
-        nc.vector.tensor_scalar_mul(s2_neg[:], s2[:], -1.0)
+        nc.vector.tensor_scalar_mul(s2_neg[0][:], s2[:], -1.0)
+        gate(s1[0], a_sb, list1[:, parts[0]])
+        nc.vector.tensor_tensor(f1[:].indirect(list3[:, parts[0]]), s1[0][:], s2_neg[0][:], ALU.add)
 
-        for h in range(2):
-            part = slice(h * LIST_COLS // 2, (h + 1) * LIST_COLS // 2)
-            nc.scalar.activation(
-                out=s1[h][:], in_=a_sb[:].indirect(list1[:, part]), func=ACT.Sigmoid,
-                bias=thr_t[:], scale=slope_t[:],
-            )
-            nc.vector.tensor_tensor(
-                f1[:].indirect(list3[:, part]), s1[h][:], s2_neg[:, h * HALF : (h + 1) * HALF], ALU.add
-            )
+        s2 = sb.tile([P, HALF], F32, name="s2", tag="s2")
+        gate(s2, b_sb, list2[:, parts[1]])
+        gate(s1[1], a_sb, list1[:, parts[1]])
+        nc.scalar.mul(s2_neg[1][:], s2[:], -1.0)
+        nc.vector.tensor_tensor(f1[:].indirect(list3[:, parts[1]]), s1[1][:], s2_neg[1][:], ALU.add)
 
         for c in range(COLS // BANK):
             cols = slice(c * BANK, (c + 1) * BANK)

@@ -34,10 +34,10 @@ def load_words(nc, tile, words):
     nc.sync.dma_start(out=tile[:].bitcast(I32), in_=words.bitcast(I32))
 
 
-def load_scales(queue, plane, scales, first_row):
+def load_scales(queues, plane, scales, first_row):
     rows = scales[0].rearrange("(g r) n -> r g n", r=PACK)
     for r in range(PACK):
-        queue.dma_start(
+        queues[r].dma_start(
             out=plane[first_row + r : P : QUADRANT, :].bitcast(I32), in_=rows[r].bitcast(I32)
         )
 
@@ -77,7 +77,6 @@ def tile_attend_gatedgap_madethree_kernel(
         a_sb = sb.tile([P, COLS], F32, name="a_sb")
         b_sb = sb.tile([P, COLS], F32, name="b_sb")
         s1 = [sb.tile([P, HALF], F32, name="s1_%d" % h) for h in range(2)]
-        s2_neg = [sb.tile([P, HALF], F32, name="s2_neg_%d" % h) for h in range(2)]
         f1 = sb.tile([P, COLS], F32, name="f1")
         cc = sb.tile([P, COLS], F32, name="cc")
         y = [sb.tile([P, HALF], F32, name="y_%d" % h) for h in range(2)]
@@ -102,16 +101,16 @@ def tile_attend_gatedgap_madethree_kernel(
             )
         load_words(nc, wq_w, wq_rows)
         load_words(nc, notes_w, notes_words[0])
-        load_scales(nc.sync, notes_s, notes_scales, 0)
+        nc.sync.dma_start(list2[:], offs2)
+        load_scales([nc.sync] * PACK, notes_s, notes_scales, 0)
         load_words(nc, keys_w, keys_words[0].rearrange("p n t -> p (n t)"))
-        load_scales(nc.sync, keys_s, keys_scales, KEYS_ROW)
         nc.gpsimd.dma_start(out=slope_t[:], in_=slope)
         nc.gpsimd.dma_start(out=thr_t[:], in_=thr)
-        nc.sync.dma_start(list2[:], offs2)
+        load_scales([nc.sync] * (PACK - 1) + [nc.gpsimd], keys_s, keys_scales, KEYS_ROW)
         nc.sync.dma_start(list1[:], offs)
         nc.sync.dma_start(list3[:], offs3)
         load_words(nc, users_w, users_words[0].rearrange("p n t -> p (n t)"))
-        load_scales(nc.sync, users_s, users_scales, USERS_ROW)
+        load_scales([nc.sync] * PACK, users_s, users_scales, USERS_ROW)
         nc.sync.dma_start(list4[:], offs4)
 
         dealt = wq_wd[:].rearrange("p (t m) -> p m t", t=PACK)
@@ -155,7 +154,7 @@ def tile_attend_gatedgap_madethree_kernel(
                 rhs=notes_w[:, 2 * cols.start : 2 * cols.stop].bitcast(FP4X4),
                 rhs_scale=notes_s[:, cols], start=True, stop=True,
             )
-            if c % 2 == 0:
+            if c % 2 == 1:
                 nc.scalar.copy(out=b_sb[:, cols], in_=b_ps[:, 0:NOTE_CHUNK])
             else:
                 nc.vector.tensor_copy(out=b_sb[:, cols], in_=b_ps[:, 0:NOTE_CHUNK])
@@ -171,22 +170,25 @@ def tile_attend_gatedgap_madethree_kernel(
         s2 = sb.tile([P, HALF], F32, name="s2", tag="s2")
         gate(s2, b_sb, list2[:, parts[0]])
 
-        for c in range(COLS // NOTE_CHUNK):
-            cols = slice(c * NOTE_CHUNK, (c + 1) * NOTE_CHUNK)
-            a_ps = ps.tile([P, BANK], F32, name="a_ps%d" % c, tag=("a0", "a1", "a2", "shared")[c])
+        edges = (0, 256, 512, 768, 896, 1024)
+        a_tags = ("a0", "a1", "a2", "shared", "b_ps0")
+        for c in range(len(a_tags)):
+            cols = slice(edges[c], edges[c + 1])
+            width = cols.stop - cols.start
+            a_ps = ps.tile([P, BANK], F32, name="a_ps%d" % c, tag=a_tags[c])
             nc.tensor.matmul_mx(
-                out=a_ps[:, 0:NOTE_CHUNK], lhsT=qv_w[:].bitcast(FP8X4), lhsT_scale=qv_s[:],
+                out=a_ps[:, 0:width], lhsT=qv_w[:].bitcast(FP8X4), lhsT_scale=qv_s[:],
                 rhs=keys_w[:, cols].bitcast(FP8X4), rhs_scale=keys_s[KEYS_ROW:P, cols],
                 start=True, stop=True,
             )
-            if c == COLS // NOTE_CHUNK - 1:
-                nc.scalar.copy(out=a_sb[:, cols], in_=a_ps[:, 0:NOTE_CHUNK])
+            if c == len(a_tags) - 1:
+                nc.scalar.copy(out=a_sb[:, cols], in_=a_ps[:, 0:width])
             else:
-                nc.vector.tensor_copy(out=a_sb[:, cols], in_=a_ps[:, 0:NOTE_CHUNK])
+                nc.vector.tensor_copy(out=a_sb[:, cols], in_=a_ps[:, 0:width])
 
         c0_ps = [
-            ps.tile([P, BANK], F32, name="c0_ps0", tag="b_ps0"),
-            ps.tile([P, BANK], F32, name="c0_ps1", tag="b_ps1"),
+            ps.tile([P, BANK], F32, name="c0_ps0", tag="a0"),
+            ps.tile([P, BANK], F32, name="c0_ps1", tag="a1"),
         ]
         for c in range(COLS // BANK):
             cols = slice(c * BANK, (c + 1) * BANK)
@@ -196,6 +198,10 @@ def tile_attend_gatedgap_madethree_kernel(
                 start=True, stop=True,
             )
 
+        s2_neg = [
+            sb.tile([P, HALF], F32, name="s2_neg_0", tag="keys_w", align_bytes=64),
+            sb.tile([P, HALF], F32, name="s2_neg_1"),
+        ]
         nc.vector.tensor_scalar_mul(s2_neg[0][:], s2[:], -1.0)
         gate(s1[0], a_sb, list1[:, parts[0]])
         nc.vector.tensor_tensor(f1[:].indirect(list3[:, parts[0]]), s1[0][:], s2_neg[0][:], ALU.add)

@@ -134,14 +134,19 @@ def tile_attend_gatedgap_madethree_kernel(
             in_=wq_w[:, K // 2 : K].bitcast(I32).rearrange("p (m t) -> p m t", t=PACK),
         )
 
-        qv_ps = ps.tile([P, BANK], F32, name="qv_ps", tag="shared")
-        for t in range(PACK):
-            cols = slice(t * P, (t + 1) * P)
-            nc.tensor.matmul_mx(
-                out=qv_ps[:, cols], lhsT=wq_wd[:, cols].bitcast(FP8X4), lhsT_scale=wq_sd[:, cols],
-                rhs=st_w[:].bitcast(FP8X4), rhs_scale=st_s[:], start=True, stop=True,
+        for pair, (tag, engine_copy) in enumerate((("a1", nc.vector.tensor_copy), ("shared", nc.scalar.copy))):
+            qv_ps = ps.tile([P, BANK], F32, name="qv_ps%d" % pair, tag=tag)
+            for e in range(2):
+                cols = slice((2 * pair + e) * P, (2 * pair + e + 1) * P)
+                nc.tensor.matmul_mx(
+                    out=qv_ps[:, e * P : (e + 1) * P], lhsT=wq_wd[:, cols].bitcast(FP8X4),
+                    lhsT_scale=wq_sd[:, cols], rhs=st_w[:].bitcast(FP8X4), rhs_scale=st_s[:],
+                    start=True, stop=True,
+                )
+            engine_copy(
+                out=qv_bf[:, :, 2 * pair : 2 * pair + 2],
+                in_=qv_ps[:, 0 : 2 * Q].rearrange("p (e q) -> p q e", e=2),
             )
-        nc.scalar.copy(out=qv_bf[:], in_=qv_ps[:].rearrange("p (t q) -> p q t", t=PACK))
         nc.vector.quantize_mx(
             out=qv_w[:].bitcast(FP8X4), scales=qv_s[:], in_=qv_bf[:].rearrange("p q t -> p (q t)")
         )

from contextlib import ExitStack

import concourse.mybir as mybir

FLOPS = 469762048

F32 = mybir.dt.float32
BF16 = mybir.dt.bfloat16
I32 = mybir.dt.int32
U32 = mybir.dt.uint32
U16 = mybir.dt.uint16
U8 = mybir.dt.uint8
FP8X4 = mybir.dt.float8_e4m3fn_x4
FP4X4 = mybir.dt.float4_e2m1fn_x4
ALU = mybir.AluOpType
ACT = mybir.ActivationFunctionType

P = 128
PACK = 4
QUADRANT = 32
K = 512
Q = 128
COLS = 1024
SLOTS = 512
HALF = SLOTS // 2
LIST_COLS = SLOTS // 16
BANK = 512
NOTE_CHUNK = 256
KEYS_ROW = 4
USERS_ROW = 8


def load_words(nc, tile, words):
    nc.sync.dma_start(out=tile[:].bitcast(I32), in_=words.bitcast(I32))


def load_scales(queues, plane, scales, first_row):
    rows = scales[0].rearrange("(g r) n -> r g n", r=PACK)
    for r in range(PACK):
        queues[r].dma_start(
            out=plane[first_row + r : P : QUADRANT, :].bitcast(I32), in_=rows[r].bitcast(I32)
        )


def tile_attend_gatedgap_madethree_kernel(
    tc, states, wq_words, wq_scales, keys_words, keys_scales, notes_words, notes_scales,
    users_words, users_scales, thr, slope, offs, offs2, offs3, offs4, out,
):
    nc = tc.nc
    with ExitStack() as ctx:
        sb = ctx.enter_context(tc.tile_pool(name="sb", bufs=1))
        ps = ctx.enter_context(tc.psum_pool(name="ps", bufs=1))

        wq_w = sb.tile([P, K], U32, name="wq_w", align_bytes=64)
        wq_s = sb.tile([P, K], U8, name="wq_s", align_bytes=64)
        wq_wd = sb.tile([P, K], U32, name="wq_wd", align_bytes=64)
        wq_sd = sb.tile([P, K], U8, name="wq_sd", align_bytes=64)
        keys_w = sb.tile([P, COLS], U32, name="keys_w", align_bytes=64)
        keys_s = sb.tile([P, COLS], U8, name="keys_s", align_bytes=64)
        notes_w = sb.tile([P, 2 * COLS], U8, name="notes_w", align_bytes=64)
        notes_s = sb.tile([P, COLS], U8, name="notes_s", align_bytes=64)
        users_w = sb.tile([P, COLS], U32, name="users_w", align_bytes=64)
        users_s = sb.tile([P, COLS], U8, name="users_s", align_bytes=64)
        st_raw = sb.tile([P, PACK, Q], F32, name="st_raw", align_bytes=64)
        st_bf = sb.tile([P, Q, PACK], BF16, name="st_bf", align_bytes=64)
        st_w = sb.tile([P, Q], U32, name="st_w", align_bytes=64)
        st_s = sb.tile([P, Q], U8, name="st_s", align_bytes=64)
        qv_bf = sb.tile([P, Q, PACK], BF16, name="qv_bf", align_bytes=64)
        qv_w = sb.tile([P, Q], U32, name="qv_w", align_bytes=64)
        qv_s = sb.tile([P, Q], U8, name="qv_s", align_bytes=64)
        thr_t = sb.tile([P, 1], F32, name="thr_t")
        slope_t = sb.tile([P, 1], F32, name="slope_t")
        list1 = sb.tile([P, LIST_COLS], U16, name="list1")
        list2 = sb.tile([P, LIST_COLS], U16, name="list2")
        list3 = sb.tile([P, LIST_COLS], U16, name="list3")
        list4 = sb.tile([P, LIST_COLS], U16, name="list4")
        a_sb = sb.tile([P, COLS], F32, name="a_sb")
        b_sb = sb.tile([P, COLS], F32, name="b_sb")
        s1 = [sb.tile([P, HALF], F32, name="s1_%d" % h) for h in range(2)]
        f1 = sb.tile([P, COLS], F32, name="f1")
        cc = sb.tile([P, COLS], F32, name="cc")
        y = [sb.tile([P, HALF], F32, name="y_%d" % h) for h in range(2)]

        warm_in = sb.tile([P, 1], F32, name="warm_in")
        warm_out = sb.tile([P, 1], F32, name="warm_out")
        nc.vector.memset(notes_s[:].bitcast(I32), 0)
        nc.vector.memset(warm_in[:], 0.0)
        nc.scalar.activation(out=warm_out[:], in_=warm_in[:], func=ACT.Sigmoid)

        for plane in (keys_s, users_s):
            nc.vector.memset(plane[:].bitcast(I32), 0)
        nc.vector.memset(f1[:], 0.0)

        wq_rows = wq_words[0].rearrange("p n t -> p (n t)")
        nc.sync.dma_start(out=st_raw[:], in_=states.rearrange("(p j) q -> p j q", j=PACK))
        for g in range(P // QUADRANT):
            rows = wq_scales[0][PACK * g : PACK * (g + 1), :].bitcast(I32)
            nc.sync.dma_start(
                out=wq_s[QUADRANT * g : QUADRANT * (g + 1), :].bitcast(I32),
                in_=rows.unsqueeze(0).to_broadcast([QUADRANT // PACK, PACK, K // 4]),
            )
        load_words(nc, wq_w, wq_rows)
        load_words(nc, notes_w, notes_words[0])
        nc.sync.dma_start(list2[:], offs2)
        load_scales([nc.sync] * PACK, notes_s, notes_scales, 0)
        load_words(nc, keys_w, keys_words[0].rearrange("p n t -> p (n t)"))
        nc.gpsimd.dma_start(out=slope_t[:], in_=slope)
        nc.gpsimd.dma_start(out=thr_t[:], in_=thr)
        load_scales([nc.sync] * (PACK - 1) + [nc.gpsimd], keys_s, keys_scales, KEYS_ROW)
        nc.sync.dma_start(list1[:], offs)
        nc.sync.dma_start(list3[:], offs3)
        load_words(nc, users_w, users_words[0].rearrange("p n t -> p (n t)"))
        load_scales([nc.sync] * PACK, users_s, users_scales, USERS_ROW)
        nc.sync.dma_start(list4[:], offs4)

        dealt = wq_wd[:].rearrange("p (t m) -> p m t", t=PACK)
        for engine_copy, rows in ((nc.vector.tensor_copy, slice(0, Q // 2)), (nc.scalar.copy, slice(Q // 2, Q))):
            engine_copy(
                out=st_bf[:, rows, :].rearrange("p (c i) t -> p c t i", i=4),
                in_=st_raw[:, :, rows].rearrange("p t (c i) -> p c t i", i=4),
            )
        nc.scalar.copy(
            out=dealt[:, 0 : P // 2, :], in_=wq_w[:, 0 : K // 2].rearrange("p (m t) -> p m t", t=PACK)
        )
        nc.vector.tensor_copy(
            out=wq_sd[:].rearrange("p (t m) -> p m t", t=PACK),
            in_=wq_s[:].rearrange("p (m t) -> p m t", t=PACK),
        )
        nc.vector.quantize_mx(
            out=st_w[:].bitcast(FP8X4), scales=st_s[:], in_=st_bf[:].rearrange("p q t -> p (q t)")
        )
        nc.vector.tensor_copy(
            out=dealt[:, P // 2 : P, :].bitcast(I32),
            in_=wq_w[:, K // 2 : K].bitcast(I32).rearrange("p (m t) -> p m t", t=PACK),
        )

        for pair, (tag, engine_copy) in enumerate((("a1", nc.vector.tensor_copy), ("shared", nc.scalar.copy))):
            qv_ps = ps.tile([P, BANK], F32, name="qv_ps%d" % pair, tag=tag)
            for e in range(2):
                cols = slice((2 * pair + e) * P, (2 * pair + e + 1) * P)
                nc.tensor.matmul_mx(
                    out=qv_ps[:, e * P : (e + 1) * P], lhsT=wq_wd[:, cols].bitcast(FP8X4),
                    lhsT_scale=wq_sd[:, cols], rhs=st_w[:].bitcast(FP8X4), rhs_scale=st_s[:],
                    start=True, stop=True,
                )
            engine_copy(
                out=qv_bf[:, :, 2 * pair : 2 * pair + 2],
                in_=qv_ps[:, 0 : 2 * Q].rearrange("p (e q) -> p q e", e=2),
            )
        nc.vector.quantize_mx(
            out=qv_w[:].bitcast(FP8X4), scales=qv_s[:], in_=qv_bf[:].rearrange("p q t -> p (q t)")
        )

        for c in range(COLS // NOTE_CHUNK):
            cols = slice(c * NOTE_CHUNK, (c + 1) * NOTE_CHUNK)
            b_ps = ps.tile([P, BANK], F32, name="b_ps%d" % c)
            nc.tensor.matmul_mx(
                out=b_ps[:, 0:NOTE_CHUNK], lhsT=qv_w[:].bitcast(FP8X4), lhsT_scale=qv_s[:],
                rhs=notes_w[:, 2 * cols.start : 2 * cols.stop].bitcast(FP4X4),
                rhs_scale=notes_s[:, cols], start=True, stop=True,
            )
            if c % 2 == 1:
                nc.scalar.copy(out=b_sb[:, cols], in_=b_ps[:, 0:NOTE_CHUNK])
            else:
                nc.vector.tensor_copy(out=b_sb[:, cols], in_=b_ps[:, 0:NOTE_CHUNK])

        parts = [slice(h * LIST_COLS // 2, (h + 1) * LIST_COLS // 2) for h in range(2)]

        def gate(dst, window, offsets):
            nc.scalar.activation(
                out=dst[:], in_=window[:].indirect(offsets), func=ACT.Sigmoid,
                bias=thr_t[:], scale=slope_t[:],
            )

        s2 = sb.tile([P, HALF], F32, name="s2", tag="s2")
        gate(s2, b_sb, list2[:, parts[0]])

        edges = (0, 256, 512, 768, 896, 1024)
        a_tags = ("a0", "a1", "a2", "shared", "b_ps0")
        for c in range(len(a_tags)):
            cols = slice(edges[c], edges[c + 1])
            width = cols.stop - cols.start
            a_ps = ps.tile([P, BANK], F32, name="a_ps%d" % c, tag=a_tags[c])
            nc.tensor.matmul_mx(
                out=a_ps[:, 0:width], lhsT=qv_w[:].bitcast(FP8X4), lhsT_scale=qv_s[:],
                rhs=keys_w[:, cols].bitcast(FP8X4), rhs_scale=keys_s[KEYS_ROW:P, cols],
                start=True, stop=True,
            )
            if c == len(a_tags) - 1:
                nc.scalar.copy(out=a_sb[:, cols], in_=a_ps[:, 0:width])
            else:
                nc.vector.tensor_copy(out=a_sb[:, cols], in_=a_ps[:, 0:width])

        c0_ps = [
            ps.tile([P, BANK], F32, name="c0_ps0", tag="a0"),
            ps.tile([P, BANK], F32, name="c0_ps1", tag="a1"),
        ]
        for c in range(COLS // BANK):
            cols = slice(c * BANK, (c + 1) * BANK)
            nc.tensor.matmul_mx(
                out=c0_ps[c][:], lhsT=st_w[:].bitcast(FP8X4), lhsT_scale=st_s[:],
                rhs=users_w[:, cols].bitcast(FP8X4), rhs_scale=users_s[USERS_ROW:P, cols],
                start=True, stop=True,
            )

        s2_neg = [
            sb.tile([P, HALF], F32, name="s2_neg_0", tag="keys_w", align_bytes=64),
            sb.tile([P, HALF], F32, name="s2_neg_1"),
        ]
        nc.vector.tensor_scalar_mul(s2_neg[0][:], s2[:], -1.0)
        gate(s1[0], a_sb, list1[:, parts[0]])
        nc.vector.tensor_tensor(f1[:].indirect(list3[:, parts[0]]), s1[0][:], s2_neg[0][:], ALU.add)

        s2 = sb.tile([P, HALF], F32, name="s2", tag="s2")
        gate(s2, b_sb, list2[:, parts[1]])
        gate(s1[1], a_sb, list1[:, parts[1]])
        nc.scalar.mul(s2_neg[1][:], s2[:], -1.0)
        nc.vector.tensor_tensor(f1[:].indirect(list3[:, parts[1]]), s1[1][:], s2_neg[1][:], ALU.add)

        for c in range(COLS // BANK):
            cols = slice(c * BANK, (c + 1) * BANK)
            nc.vector.scalar_tensor_tensor(
                out=cc[:, cols], in0=f1[:, cols], scalar=3.0, in1=c0_ps[c][:], op0=ALU.mult, op1=ALU.add
            )

        nc.vector.tensor_copy(y[0][:], cc[:].indirect(list4[:, 0 : LIST_COLS // 2]))
        nc.sync.dma_start(out=out[:, 0:HALF], in_=y[0][:])
        nc.scalar.activation(
            out=y[1][:], in_=cc[:].indirect(list4[:, LIST_COLS // 2 : LIST_COLS]), func=ACT.Copy
        )
        nc.scalar.dma_start(out=out[:, HALF:SLOTS], in_=y[1][:])
